import numpy as np
import ml_dtypes


def mxq(x, axis, fmt="e4m3"):
    dtype, down = {"e4m3": (ml_dtypes.float8_e4m3fn, 7), "e5m2": (ml_dtypes.float8_e5m2, 14)}[fmt]
    v = np.moveaxis(np.asarray(x, np.float32).astype(ml_dtypes.bfloat16).astype(np.float64), axis, -1)
    blocks = v.reshape(v.shape[:-1] + (-1, 32))
    amax = np.abs(blocks).max(-1, keepdims=True)
    byte = np.maximum(np.where(amax > 0, np.frexp(amax)[1] - 1 + 127, 0) - down, 1)
    scale = np.exp2(byte - 127.0)
    codes = (blocks / scale).astype(np.float32).astype(dtype).astype(np.float64)
    return np.moveaxis((codes * scale).reshape(v.shape), -1, axis)


WIDE = False


def mx_kscale(k):
    if not WIDE:
        return np.ones(k)
    levels = np.array([10, -10, 5, -5, 0])
    if k % 512:
        return np.exp2(np.random.permutation(np.resize(levels, k // 32))).repeat(32)
    a = np.empty((k // 512, 16))
    for p in range(k // 512):
        a[p, :8] = np.random.permutation(np.resize(levels, 8))
        for g in range(8):
            far = levels[np.abs(levels - a[p, g]) >= 10]
            a[p, g + 8] = far[np.random.randint(len(far))]
    return np.exp2(a.ravel()).repeat(32)


def f64(x):
    return np.asarray(x).astype(np.float64)


def striped(idx):
    return np.tile(idx.reshape(-1, 16).T, (8, 1)).astype(np.uint16)


def unstriped(offs):
    return offs[:16].T.reshape(-1).astype(np.int64)

def planes(y):
    n, m = y.shape
    v = y.astype(np.float32).astype(ml_dtypes.bfloat16).astype(np.float64).reshape(n // 32, 32, m)
    top = np.abs(v).max(1)
    byte = np.clip(np.where(top > 0, np.frexp(top)[1] - 1 + 127 - 7, 1), 1, 254)
    codes = (v * np.exp2(127.0 - byte)[:, None, :]).reshape(n, m).astype(np.float32).astype(ml_dtypes.float8_e4m3fn).view(np.uint8)
    words = codes.reshape(n // 512, 128, 4, m).transpose(0, 1, 3, 2)
    return np.ascontiguousarray(words), np.ascontiguousarray(byte.astype(np.uint8).reshape(n // 512, 16, m))


K, T, S, N = 512, 1024, 512, 512


def setup_inputs():
    n = np.random.standard_normal
    s = mx_kscale(K)[:, None]
    return {
        "xT": (n((K, T)) * s).astype(np.float32),
        "w1": (n((K, N)) / np.sqrt(K) / s).astype(np.float32),
        "w2": (n((K, N)) / np.sqrt(K) / s).astype(np.float32),
        "w3": (n((K, N)) / np.sqrt(K) / s).astype(np.float32),
        "offs": striped(np.random.permutation(T)[:S]),
    }


def reference(xT, w1, w2, w3, offs):
    xq = mxq(f64(xT)[:, unstriped(offs)], 0, "e4m3")
    out_0 = np.maximum(np.maximum(mxq(f64(w1), 0, "e4m3").T @ xq, mxq(f64(w2), 0, "e4m3").T @ xq), mxq(f64(w3), 0, "e4m3").T @ xq)
    return (out_0,) + planes(out_0)

@@ -1,0 +1,148 @@
+from contextlib import ExitStack
+
+import concourse.mybir as mybir
+
+K, T, S, N = 512, 1024, 512, 512
+FLOPS = 3 * 2 * K * N * S
+
+F32 = mybir.dt.float32
+BF16 = mybir.dt.bfloat16
+I32 = mybir.dt.int32
+U32 = mybir.dt.uint32
+U16 = mybir.dt.uint16
+U8 = mybir.dt.uint8
+FP8X4 = mybir.dt.float8_e4m3fn_x4
+
+P = 128
+PACK = 4
+HALF = 256
+
+
+def copy_on(nc, engine, out, in_):
+    if engine == "scalar":
+        nc.scalar.copy(out=out, in_=in_)
+    elif engine == "vector":
+        nc.vector.tensor_copy(out=out, in_=in_)
+    else:
+        nc.gpsimd.tensor_scalar(out, in_, 1.0, 0.0, mybir.AluOpType.mult, mybir.AluOpType.add)
+
+
+def interleave(nc, engine, grouped, planes):
+    copy_on(
+        nc, engine,
+        grouped.rearrange("p (c i) r -> p c r i", i=4),
+        planes.rearrange("p r (c i) -> p c r i", i=4),
+    )
+
+
+def tile_picked_maxout_max_lo_kernel(tc, xT, w1, w2, w3, offs, out_0, out_1, out_2):
+    nc = tc.nc
+    with ExitStack() as ctx:
+        keep = ctx.enter_context(tc.tile_pool(name="keep", bufs=1))
+        psum = ctx.enter_context(tc.psum_pool(name="psum", bufs=1))
+
+        x_rows = xT.rearrange("(p r) t -> p r t", r=PACK)
+        offsets = keep.tile([P, S // 16], U16, name="offsets")
+        x_raw = [keep.tile([P, T], F32, name=f"x_raw{r}") for r in range(PACK)]
+        nc.sync.dma_start(x_raw[0][:], x_rows[:, 0, :])
+        nc.sync.dma_start(offsets[:], offs)
+        for r in range(1, PACK):
+            nc.sync.dma_start(x_raw[r][:], x_rows[:, r, :])
+        w_raw = []
+        for i, w in enumerate((w1, w2, w3)):
+            w_rows = w.rearrange("(p r) n -> p r n", r=PACK)
+            halves = [keep.tile([P, PACK, HALF], F32, name=f"w_raw{i}{h}") for h in range(2)]
+            for h in range(2):
+                nc.sync.dma_start(halves[h][:], w_rows[:, :, h * HALF : (h + 1) * HALF])
+            w_raw.append(halves)
+
+        picked = [keep.tile([P, PACK, HALF], F32, name=f"picked{c}") for c in range(2)]
+        for r in range(PACK):
+            for c in range(2):
+                nc.vector.tensor_copy(picked[c][:, r, :], x_raw[r][:].indirect(offsets[:, c * 16 : (c + 1) * 16]))
+
+        x_codes = keep.tile([P, S], U32, name="x_codes", align_bytes=64)
+        x_scales = keep.tile([P, S], U8, name="x_scales", align_bytes=64)
+        x_bf = [keep.tile([P, HALF, PACK], BF16, name=f"x_bf{c}", align_bytes=64) for c in range(2)]
+        for c, engine in enumerate(("scalar", "vector")):
+            interleave(nc, engine, x_bf[c][:], picked[c][:])
+        for c in (0, 1):
+            cols = slice(c * HALF, (c + 1) * HALF)
+            nc.vector.quantize_mx(out=x_codes[:, cols].bitcast(FP8X4), scales=x_scales[:, cols], in_=x_bf[c][:].rearrange("p c r -> p (c r)"))
+
+        w_codes = [keep.tile([P, N], U32, name=f"w_codes{i}", align_bytes=64) for i in range(3)]
+        w_scales = [keep.tile([P, N], U8, name=f"w_scales{i}", align_bytes=64) for i in range(3)]
+        w_bf = {}
+
+        def round_weights(i, h, engine, tag):
+            w_bf[i, h] = keep.tile([P, PACK, 64, PACK], BF16, name=f"w_bf{i}{h}", tag=tag, align_bytes=64)
+            copy_on(
+                nc, engine,
+                w_bf[i, h][:].rearrange("p t m r -> p m r t"),
+                w_raw[i][h][:].rearrange("p r (m t) -> p m r t", t=PACK),
+            )
+
+        def quantise_weights(i):
+            for t in range(PACK):
+                for h in range(2):
+                    cols = slice(t * P + h * 64, t * P + (h + 1) * 64)
+                    nc.vector.quantize_mx(out=w_codes[i][:, cols].bitcast(FP8X4), scales=w_scales[i][:, cols], in_=w_bf[i, h][:, t].rearrange("p m r -> p (m r)"))
+
+        y = [keep.tile([P, PACK, HALF], F32, name=f"y{c}") for c in range(2)]
+
+        def multiply(i):
+            banks = {}
+            for c in range(2):
+                for u in range(2):
+                    banks[c, u] = psum.tile([P, 2, HALF], F32, name=f"bank{i}{c}{u}", tag=f"bank{i % 2}{c}{u}")
+                    for e in range(2):
+                        t = 2 * u + e
+                        nc.tensor.matmul_mx(
+                            out=banks[c, u][:, e, :],
+                            lhsT=w_codes[i][:, t * P : (t + 1) * P].bitcast(FP8X4),
+                            lhsT_scale=w_scales[i][:, t * P : (t + 1) * P],
+                            rhs=x_codes[:, c * HALF : (c + 1) * HALF].bitcast(FP8X4),
+                            rhs_scale=x_scales[:, c * HALF : (c + 1) * HALF],
+                            start=True, stop=True,
+                        )
+            return banks
+
+        round_weights(0, 0, "scalar", "wa0")
+        round_weights(0, 1, "vector", "wb0")
+        quantise_weights(0)
+        banks = multiply(0)
+        round_weights(1, 0, "scalar", "wa1")
+        round_weights(1, 1, "vector", "wb1")
+        for (c, u), bank in banks.items():
+            nc.scalar.copy(out=y[c][:, 2 * u : 2 * u + 2, :], in_=bank[:])
+        quantise_weights(1)
+        banks = multiply(1)
+        round_weights(2, 0, "scalar", "wa2")
+        for (c, u), bank in banks.items():
+            part = y[c][:, 2 * u : 2 * u + 2, :]
+            nc.vector.tensor_tensor(part, bank[:], part, mybir.AluOpType.max)
+        round_weights(2, 1, "vector", "wb2")
+        quantise_weights(2)
+        banks = multiply(2)
+
+        y_rows = out_0.rearrange("(p t) s -> p t s", t=PACK)
+        for (c, u), bank in banks.items():
+            part = y[c][:, 2 * u : 2 * u + 2, :]
+            nc.vector.tensor_tensor(part, bank[:], part, mybir.AluOpType.max)
+            nc.sync.dma_start(y_rows[:, 2 * u : 2 * u + 2, c * HALF : (c + 1) * HALF], part)
+
+        y_codes = keep.tile([P, S], U32, name="y_codes", align_bytes=64)
+        y_scales = keep.tile([P, S], U8, name="y_scales", align_bytes=64)
+        y_bf = [keep.tile([P, HALF, PACK], BF16, name=f"y_bf{c}", align_bytes=64) for c in range(2)]
+        words = out_1[0].rearrange("p s r -> p (s r)").bitcast(I32)
+        interleave(nc, "scalar", y_bf[0][:], y[0][:])
+        interleave(nc, "scalar", y_bf[1][:, 0:128, :], y[1][:, :, 0:128])
+        for c in range(2):
+            cols = slice(c * HALF, (c + 1) * HALF)
+            if c == 1:
+                interleave(nc, "vector", y_bf[1][:, 128:256, :], y[1][:, :, 128:256])
+            nc.vector.quantize_mx(out=y_codes[:, cols].bitcast(FP8X4), scales=y_scales[:, cols], in_=y_bf[c][:].rearrange("p c r -> p (c r)"))
+            nc.sync.dma_start(words[:, cols], y_codes[:, cols].bitcast(I32))
+        for q in range(4):
+            queue = nc.scalar if q % 2 == 0 else nc.sync
+            queue.dma_start(out_2[0, 4 * q : 4 * q + 4, :].bitcast(I32), y_scales[32 * q : 32 * q + 4, :].bitcast(I32))

@@ -48,45 +48,42 @@ def tile_picked_maxout_max_lo_kernel(tc, xT, w1, w2, w3, offs, out_0, out_1, out
         nc.sync.dma_start(offsets[:], offs)
         for r in range(1, PACK):
             nc.sync.dma_start(x_raw[r][:], x_rows[:, r, :])
-        w_raw = []
+        w_raw = [keep.tile([P, PACK, N], F32, name=f"w_raw{i}") for i in range(3)]
         for i, w in enumerate((w1, w2, w3)):
-            w_rows = w.rearrange("(p r) n -> p r n", r=PACK)
-            halves = [keep.tile([P, PACK, HALF], F32, name=f"w_raw{i}{h}") for h in range(2)]
-            for h in range(2):
-                nc.sync.dma_start(halves[h][:], w_rows[:, :, h * HALF : (h + 1) * HALF])
-            w_raw.append(halves)
+            nc.sync.dma_start(w_raw[i][:], w.rearrange("(p r) n -> p r n", r=PACK))
 
-        picked = [keep.tile([P, PACK, HALF], F32, name=f"picked{c}") for c in range(2)]
-        for r in range(PACK):
-            for c in range(2):
-                nc.vector.tensor_copy(picked[c][:, r, :], x_raw[r][:].indirect(offsets[:, c * 16 : (c + 1) * 16]))
+        picked = keep.tile([P, PACK, S], F32, name="picked")
+        for r in range(PACK - 1):
+            nc.vector.tensor_copy(picked[:, r, :], x_raw[r][:].indirect(offsets[:]))
+        for g in range(4):
+            nc.vector.tensor_copy(picked[:, PACK - 1, g * 128 : (g + 1) * 128], x_raw[PACK - 1][:].indirect(offsets[:, g * 8 : (g + 1) * 8]))
 
         x_codes = keep.tile([P, S], U32, name="x_codes", align_bytes=64)
         x_scales = keep.tile([P, S], U8, name="x_scales", align_bytes=64)
-        x_bf = [keep.tile([P, HALF, PACK], BF16, name=f"x_bf{c}", align_bytes=64) for c in range(2)]
-        for c, engine in enumerate(("scalar", "vector")):
-            interleave(nc, engine, x_bf[c][:], picked[c][:])
-        for c in (0, 1):
+        x_bf = keep.tile([P, S, PACK], BF16, name="x_bf", align_bytes=64)
+        for g, engine in enumerate(("scalar", "scalar", "scalar", "vector")):
+            interleave(nc, engine, x_bf[:, g * 128 : (g + 1) * 128, :], picked[:, :, g * 128 : (g + 1) * 128])
+        for c in range(2):
             cols = slice(c * HALF, (c + 1) * HALF)
-            nc.vector.quantize_mx(out=x_codes[:, cols].bitcast(FP8X4), scales=x_scales[:, cols], in_=x_bf[c][:].rearrange("p c r -> p (c r)"))
+            nc.vector.quantize_mx(out=x_codes[:, cols].bitcast(FP8X4), scales=x_scales[:, cols], in_=x_bf[:, cols, :].rearrange("p c r -> p (c r)"))
 
         w_codes = [keep.tile([P, N], U32, name=f"w_codes{i}", align_bytes=64) for i in range(3)]
         w_scales = [keep.tile([P, N], U8, name=f"w_scales{i}", align_bytes=64) for i in range(3)]
         w_bf = {}
 
-        def round_weights(i, h, engine, tag):
-            w_bf[i, h] = keep.tile([P, PACK, 64, PACK], BF16, name=f"w_bf{i}{h}", tag=tag, align_bytes=64)
-            copy_on(
-                nc, engine,
-                w_bf[i, h][:].rearrange("p t m r -> p m r t"),
-                w_raw[i][h][:].rearrange("p r (m t) -> p m r t", t=PACK),
-            )
+        def round_weights(i, shares, tag):
+            w_bf[i] = keep.tile([P, PACK, P, PACK], BF16, name=f"w_bf{i}", tag=tag, align_bytes=64)
+            for engine, m0, m1 in shares:
+                copy_on(
+                    nc, engine,
+                    w_bf[i][:, :, m0:m1, :].rearrange("p t m r -> p m t r" if engine == "gpsimd" else "p t m r -> p m r t"),
+                    w_raw[i][:, :, PACK * m0 : PACK * m1].rearrange("p r (m t) -> p m t r" if engine == "gpsimd" else "p r (m t) -> p m r t", t=PACK),
+                )
 
         def quantise_weights(i):
             for t in range(PACK):
-                for h in range(2):
-                    cols = slice(t * P + h * 64, t * P + (h + 1) * 64)
-                    nc.vector.quantize_mx(out=w_codes[i][:, cols].bitcast(FP8X4), scales=w_scales[i][:, cols], in_=w_bf[i, h][:, t].rearrange("p m r -> p (m r)"))
+                cols = slice(t * P, (t + 1) * P)
+                nc.vector.quantize_mx(out=w_codes[i][:, cols].bitcast(FP8X4), scales=w_scales[i][:, cols], in_=w_bf[i][:, t].rearrange("p m r -> p (m r)"))
 
         y = [keep.tile([P, PACK, HALF], F32, name=f"y{c}") for c in range(2)]
 
@@ -107,21 +104,18 @@ def tile_picked_maxout_max_lo_kernel(tc, xT, w1, w2, w3, offs, out_0, out_1, out
                         )
             return banks
 
-        round_weights(0, 0, "scalar", "wa0")
-        round_weights(0, 1, "vector", "wb0")
+        round_weights(0, [("scalar", 0, 48), ("vector", 48, 128)], "w_bf0")
         quantise_weights(0)
         banks = multiply(0)
-        round_weights(1, 0, "scalar", "wa1")
-        round_weights(1, 1, "vector", "wb1")
+        round_weights(1, [("scalar", 0, 48), ("vector", 48, 128)], "w_bf1")
         for (c, u), bank in banks.items():
             nc.scalar.copy(out=y[c][:, 2 * u : 2 * u + 2, :], in_=bank[:])
         quantise_weights(1)
         banks = multiply(1)
-        round_weights(2, 0, "scalar", "wa2")
         for (c, u), bank in banks.items():
             part = y[c][:, 2 * u : 2 * u + 2, :]
             nc.vector.tensor_tensor(part, bank[:], part, mybir.AluOpType.max)
-        round_weights(2, 1, "vector", "wb2")
+        round_weights(2, [("gpsimd", 0, 72), ("scalar", 72, 128)], "w_bf1")
         quantise_weights(2)
         banks = multiply(2)
 
@@ -137,10 +131,9 @@ def tile_picked_maxout_max_lo_kernel(tc, xT, w1, w2, w3, offs, out_0, out_1, out
         words = out_1[0].rearrange("p s r -> p (s r)").bitcast(I32)
         interleave(nc, "scalar", y_bf[0][:], y[0][:])
         interleave(nc, "scalar", y_bf[1][:, 0:128, :], y[1][:, :, 0:128])
+        interleave(nc, "vector", y_bf[1][:, 128:256, :], y[1][:, :, 128:256])
         for c in range(2):
             cols = slice(c * HALF, (c + 1) * HALF)
-            if c == 1:
-                interleave(nc, "vector", y_bf[1][:, 128:256, :], y[1][:, :, 128:256])
             nc.vector.quantize_mx(out=y_codes[:, cols].bitcast(FP8X4), scales=y_scales[:, cols], in_=y_bf[c][:].rearrange("p c r -> p (c r)"))
             nc.sync.dma_start(words[:, cols], y_codes[:, cols].bitcast(I32))
         for q in range(4):

@@ -16,6 +16,7 @@ FP8X4 = mybir.dt.float8_e4m3fn_x4
 P = 128
 PACK = 4
 HALF = 256
+BANKS = ((0, 1, 2, 0), (3, 4, 5, 6), (7, 1, 2, 3))
 
 
 def copy_on(nc, engine, out, in_):
@@ -48,7 +49,7 @@ def tile_picked_maxout_max_lo_kernel(tc, xT, w1, w2, w3, offs, out_0, out_1, out
         nc.sync.dma_start(offsets[:], offs)
         for r in range(1, PACK):
             nc.sync.dma_start(x_raw[r][:], x_rows[:, r, :])
-        w_raw = [keep.tile([P, PACK, N], F32, name=f"w_raw{i}") for i in range(3)]
+        w_raw = [keep.tile([P, PACK, N], F32, name=f"w_raw{i}", tag=f"w_raw{i}", align_bytes=64) for i in range(3)]
         for i, w in enumerate((w1, w2, w3)):
             nc.sync.dma_start(w_raw[i][:], w.rearrange("(p r) n -> p r n", r=PACK))
 
@@ -58,14 +59,18 @@ def tile_picked_maxout_max_lo_kernel(tc, xT, w1, w2, w3, offs, out_0, out_1, out
         for g in range(4):
             nc.vector.tensor_copy(picked[:, PACK - 1, g * 128 : (g + 1) * 128], x_raw[PACK - 1][:].indirect(offsets[:, g * 8 : (g + 1) * 8]))
 
-        x_codes = keep.tile([P, S], U32, name="x_codes", align_bytes=64)
+        x_codes = {}
         x_scales = keep.tile([P, S], U8, name="x_scales", align_bytes=64)
         x_bf = keep.tile([P, S, PACK], BF16, name="x_bf", align_bytes=64)
-        for g, engine in enumerate(("scalar", "scalar", "scalar", "vector")):
+        for g, engine in enumerate(("scalar", "scalar", "vector", "vector")):
             interleave(nc, engine, x_bf[:, g * 128 : (g + 1) * 128, :], picked[:, :, g * 128 : (g + 1) * 128])
-        for c in range(2):
+
+        def quantise_tokens(c, tag):
             cols = slice(c * HALF, (c + 1) * HALF)
-            nc.vector.quantize_mx(out=x_codes[:, cols].bitcast(FP8X4), scales=x_scales[:, cols], in_=x_bf[:, cols, :].rearrange("p c r -> p (c r)"))
+            x_codes[c] = keep.tile([P, HALF], U32, name=f"x_codes{c}", tag=tag, align_bytes=64)
+            nc.vector.quantize_mx(out=x_codes[c][:].bitcast(FP8X4), scales=x_scales[:, cols], in_=x_bf[:, cols, :].rearrange("p c r -> p (c r)"))
+
+        quantise_tokens(0, "x_codes0")
 
         w_codes = [keep.tile([P, N], U32, name=f"w_codes{i}", align_bytes=64) for i in range(3)]
         w_scales = [keep.tile([P, N], U8, name=f"w_scales{i}", align_bytes=64) for i in range(3)]
@@ -80,62 +85,87 @@ def tile_picked_maxout_max_lo_kernel(tc, xT, w1, w2, w3, offs, out_0, out_1, out
                     w_raw[i][:, :, PACK * m0 : PACK * m1].rearrange("p r (m t) -> p m t r" if engine == "gpsimd" else "p r (m t) -> p m r t", t=PACK),
                 )
 
-        def quantise_weights(i):
-            for t in range(PACK):
-                cols = slice(t * P, (t + 1) * P)
-                nc.vector.quantize_mx(out=w_codes[i][:, cols].bitcast(FP8X4), scales=w_scales[i][:, cols], in_=w_bf[i][:, t].rearrange("p m r -> p (m r)"))
+        def quantise_weights(i, pairs=range(2)):
+            for u in pairs:
+                cols = slice(2 * u * P, 2 * (u + 1) * P)
+                nc.vector.quantize_mx(out=w_codes[i][:, cols].bitcast(FP8X4), scales=w_scales[i][:, cols], in_=w_bf[i][:, 2 * u : 2 * u + 2].rearrange("p t m r -> p (t m r)"))
 
-        y = [keep.tile([P, PACK, HALF], F32, name=f"y{c}") for c in range(2)]
 
-        def multiply(i):
+        def product(bank_part, i, t, tokens):
+            nc.tensor.matmul_mx(
+                out=bank_part,
+                lhsT=w_codes[i][:, t * P : (t + 1) * P].bitcast(FP8X4),
+                lhsT_scale=w_scales[i][:, t * P : (t + 1) * P],
+                rhs=x_codes[tokens.start // HALF][:, tokens.start % HALF : (tokens.stop - 1) % HALF + 1].bitcast(FP8X4),
+                rhs_scale=x_scales[:, tokens],
+                start=True, stop=True,
+            )
+
+        def multiply(i, parts):
             banks = {}
-            for c in range(2):
-                for u in range(2):
-                    banks[c, u] = psum.tile([P, 2, HALF], F32, name=f"bank{i}{c}{u}", tag=f"bank{i % 2}{c}{u}")
+            for c, u in parts:
+                if True:
+                    banks[c, u] = psum.tile([P, 2, HALF], F32, name=f"bank{i}{c}{u}", tag=f"bank{BANKS[i][2 * c + u]}")
                     for e in range(2):
-                        t = 2 * u + e
-                        nc.tensor.matmul_mx(
-                            out=banks[c, u][:, e, :],
-                            lhsT=w_codes[i][:, t * P : (t + 1) * P].bitcast(FP8X4),
-                            lhsT_scale=w_scales[i][:, t * P : (t + 1) * P],
-                            rhs=x_codes[:, c * HALF : (c + 1) * HALF].bitcast(FP8X4),
-                            rhs_scale=x_scales[:, c * HALF : (c + 1) * HALF],
-                            start=True, stop=True,
-                        )
+                        product(banks[c, u][:, e, :], i, 2 * u + e, slice(c * HALF, (c + 1) * HALF))
             return banks
 
-        round_weights(0, [("scalar", 0, 48), ("vector", 48, 128)], "w_bf0")
+        def take_max(part, bank):
+            nc.vector.tensor_tensor(part, bank, part, mybir.AluOpType.max)
+
+        round_weights(0, [("scalar", 0, 56), ("vector", 56, 128)], "w_bf0")
         quantise_weights(0)
-        banks = multiply(0)
+        quantise_tokens(1, "w_raw0")
+        banks = multiply(0, ((0, 0), (0, 1), (1, 0)))
         round_weights(1, [("scalar", 0, 48), ("vector", 48, 128)], "w_bf1")
+        y_all = keep.tile([P, 2, PACK, HALF], F32, name="y_all", tag="w_raw1", align_bytes=64)
+        y = [y_all[:, c] for c in range(2)]
         for (c, u), bank in banks.items():
             nc.scalar.copy(out=y[c][:, 2 * u : 2 * u + 2, :], in_=bank[:])
         quantise_weights(1)
-        banks = multiply(1)
-        for (c, u), bank in banks.items():
-            part = y[c][:, 2 * u : 2 * u + 2, :]
-            nc.vector.tensor_tensor(part, bank[:], part, mybir.AluOpType.max)
-        round_weights(2, [("gpsimd", 0, 72), ("scalar", 72, 128)], "w_bf1")
-        quantise_weights(2)
-        banks = multiply(2)
+        banks = multiply(1, ((0, 0),))
+        nc.scalar.copy(out=y[1][:, 2:4, :], in_=multiply(0, ((1, 1),))[1, 1][:])
+        banks = {**banks, **multiply(1, ((0, 1), (1, 0), (1, 1)))}
+        for (c, u) in ((0, 0), (0, 1), (1, 0)):
+            take_max(y[c][:, 2 * u : 2 * u + 2, :], banks[c, u][:])
+        round_weights(2, [("gpsimd", 0, 100), ("scalar", 100, 128)], "w_bf1")
+        quantise_weights(2, (0,))
+        take_max(y[1][:, 2:4, :], banks[1, 1][:])
+        quantise_weights(2, (1,))
 
         y_rows = out_0.rearrange("(p t) s -> p t s", t=PACK)
-        for (c, u), bank in banks.items():
-            part = y[c][:, 2 * u : 2 * u + 2, :]
-            nc.vector.tensor_tensor(part, bank[:], part, mybir.AluOpType.max)
-            nc.sync.dma_start(y_rows[:, 2 * u : 2 * u + 2, c * HALF : (c + 1) * HALF], part)
-
         y_codes = keep.tile([P, S], U32, name="y_codes", align_bytes=64)
         y_scales = keep.tile([P, S], U8, name="y_scales", align_bytes=64)
-        y_bf = [keep.tile([P, HALF, PACK], BF16, name=f"y_bf{c}", align_bytes=64) for c in range(2)]
+        y_bf = [keep.tile([P, width, PACK], BF16, name=f"y_bf{g}", align_bytes=64) for g, width in enumerate((HALF, P, P))]
         words = out_1[0].rearrange("p s r -> p (s r)").bitcast(I32)
-        interleave(nc, "scalar", y_bf[0][:], y[0][:])
-        interleave(nc, "scalar", y_bf[1][:, 0:128, :], y[1][:, :, 0:128])
-        interleave(nc, "vector", y_bf[1][:, 128:256, :], y[1][:, :, 128:256])
-        for c in range(2):
-            cols = slice(c * HALF, (c + 1) * HALF)
-            nc.vector.quantize_mx(out=y_codes[:, cols].bitcast(FP8X4), scales=y_scales[:, cols], in_=y_bf[c][:].rearrange("p c r -> p (c r)"))
-            nc.sync.dma_start(words[:, cols], y_codes[:, cols].bitcast(I32))
+
+        banks = multiply(2, ((0, 0), (0, 1)))
+        quarters = []
+        for g in range(2):
+            bank = psum.tile([P, PACK, P], F32, name=f"quarter{g}", tag=f"bank{BANKS[2][2 + g]}")
+            for t in range(PACK):
+                product(bank[:, t, :], 2, t, slice(HALF + g * P, HALF + (g + 1) * P))
+            quarters.append(bank)
+        for u in range(2):
+            part = y[0][:, 2 * u : 2 * u + 2, :]
+            take_max(part, banks[0, u][:])
+            nc.sync.dma_start(y_rows[:, 2 * u : 2 * u + 2, 0:HALF], part)
+        interleave(nc, "scalar", y_bf[0][:], y[0])
+        for g in range(2):
+            part = y[1][:, :, g * P : (g + 1) * P]
+            take_max(part, quarters[g][:])
+            nc.sync.dma_start(y_rows[:, :, HALF + g * P : HALF + (g + 1) * P], part)
+        interleave(nc, "scalar", y_bf[1][:], y[1][:, :, 0:P])
+        interleave(nc, "vector", y_bf[2][:], y[1][:, :, P:HALF])
+
+        def quantise_result(g, cols):
+            nc.vector.quantize_mx(out=y_codes[:, cols].bitcast(FP8X4), scales=y_scales[:, cols], in_=y_bf[g][:].rearrange("p c r -> p (c r)"))
+
+        quantise_result(0, slice(0, HALF))
+        nc.sync.dma_start(words[:, 0:HALF], y_codes[:, 0:HALF].bitcast(I32))
+        quantise_result(2, slice(HALF + P, S))
+        quantise_result(1, slice(HALF, HALF + P))
+        nc.sync.dma_start(words[:, HALF:S], y_codes[:, HALF:S].bitcast(I32))
         for q in range(4):
             queue = nc.scalar if q % 2 == 0 else nc.sync
             queue.dma_start(out_2[0, 4 * q : 4 * q + 4, :].bitcast(I32), y_scales[32 * q : 32 * q + 4, :].bitcast(I32))

@@ -16,6 +16,7 @@ FP8X4 = mybir.dt.float8_e4m3fn_x4
 P = 128
 PACK = 4
 HALF = 256
+LOADS = (((0, 128),), ((0, 64), (64, 128)), ((0, 64), (64, 128)))
 BANKS = ((0, 1, 2, 0), (3, 4, 5, 6), (7, 1, 2, 3))
 
 
@@ -49,9 +50,11 @@ def tile_picked_maxout_max_lo_kernel(tc, xT, w1, w2, w3, offs, out_0, out_1, out
         nc.sync.dma_start(offsets[:], offs)
         for r in range(1, PACK):
             nc.sync.dma_start(x_raw[r][:], x_rows[:, r, :])
-        w_raw = [keep.tile([P, PACK, N], F32, name=f"w_raw{i}", tag=f"w_raw{i}", align_bytes=64) for i in range(3)]
+        w_raw = {}
         for i, w in enumerate((w1, w2, w3)):
-            nc.sync.dma_start(w_raw[i][:], w.rearrange("(p r) n -> p r n", r=PACK))
+            for m0, m1 in LOADS[i]:
+                w_raw[i, m0] = keep.tile([P, PACK, PACK * (m1 - m0)], F32, name=f"w_raw{i}_{m0}", tag=f"w_raw{i}_{m0}", align_bytes=64)
+                nc.sync.dma_start(w_raw[i, m0][:], w.rearrange("(p r) n -> p r n", r=PACK)[:, :, PACK * m0 : PACK * m1])
 
         picked = keep.tile([P, PACK, S], F32, name="picked")
         for r in range(PACK - 1):
@@ -79,10 +82,11 @@ def tile_picked_maxout_max_lo_kernel(tc, xT, w1, w2, w3, offs, out_0, out_1, out
         def round_weights(i, shares, tag):
             w_bf[i] = keep.tile([P, PACK, P, PACK], BF16, name=f"w_bf{i}", tag=tag, align_bytes=64)
             for engine, m0, m1 in shares:
+                first = max(a for a, b in LOADS[i] if a <= m0)
                 copy_on(
                     nc, engine,
                     w_bf[i][:, :, m0:m1, :].rearrange("p t m r -> p m t r" if engine == "gpsimd" else "p t m r -> p m r t"),
-                    w_raw[i][:, :, PACK * m0 : PACK * m1].rearrange("p r (m t) -> p m t r" if engine == "gpsimd" else "p r (m t) -> p m r t", t=PACK),
+                    w_raw[i, first][:, :, PACK * (m0 - first) : PACK * (m1 - first)].rearrange("p r (m t) -> p m t r" if engine == "gpsimd" else "p r (m t) -> p m r t", t=PACK),
                 )
 
         def quantise_weights(i, pairs=range(2)):
@@ -115,10 +119,10 @@ def tile_picked_maxout_max_lo_kernel(tc, xT, w1, w2, w3, offs, out_0, out_1, out
 
         round_weights(0, [("scalar", 0, 56), ("vector", 56, 128)], "w_bf0")
         quantise_weights(0)
-        quantise_tokens(1, "w_raw0")
+        quantise_tokens(1, "w_raw0_0")
         banks = multiply(0, ((0, 0), (0, 1), (1, 0)))
-        round_weights(1, [("scalar", 0, 48), ("vector", 48, 128)], "w_bf1")
-        y_all = keep.tile([P, 2, PACK, HALF], F32, name="y_all", tag="w_raw1", align_bytes=64)
+        round_weights(1, [("scalar", 0, 64), ("scalar", 64, 76), ("vector", 76, 128)], "w_bf1")
+        y_all = keep.tile([P, 2, PACK, HALF], F32, name="y_all", tag="w_raw1_64", align_bytes=64)
         y = [y_all[:, c] for c in range(2)]
         for (c, u), bank in banks.items():
             nc.scalar.copy(out=y[c][:, 2 * u : 2 * u + 2, :], in_=bank[:])
@@ -128,7 +132,7 @@ def tile_picked_maxout_max_lo_kernel(tc, xT, w1, w2, w3, offs, out_0, out_1, out
         banks = {**banks, **multiply(1, ((0, 1), (1, 0), (1, 1)))}
         for (c, u) in ((0, 0), (0, 1), (1, 0)):
             take_max(y[c][:, 2 * u : 2 * u + 2, :], banks[c, u][:])
-        round_weights(2, [("gpsimd", 0, 100), ("scalar", 100, 128)], "w_bf1")
+        round_weights(2, [("gpsimd", 0, 64), ("gpsimd", 64, 92), ("scalar", 92, 128)], "w_bf1")
         quantise_weights(2, (0,))
         take_max(y[1][:, 2:4, :], banks[1, 1][:])
         quantise_weights(2, (1,))

@@ -30,6 +30,9 @@ def copy_on(nc, engine, out, in_):
 
 
 def interleave(nc, engine, grouped, planes):
+    if engine == "gpsimd":
+        copy_on(nc, engine, grouped, planes.rearrange("p r c -> p c r"))
+        return
     copy_on(
         nc, engine,
         grouped.rearrange("p (c i) r -> p c r i", i=4),
@@ -89,10 +92,10 @@ def tile_picked_maxout_max_lo_kernel(tc, xT, w1, w2, w3, offs, out_0, out_1, out
                     w_raw[i, first][:, :, PACK * (m0 - first) : PACK * (m1 - first)].rearrange("p r (m t) -> p m t r" if engine == "gpsimd" else "p r (m t) -> p m r t", t=PACK),
                 )
 
-        def quantise_weights(i, pairs=range(2)):
-            for u in pairs:
-                cols = slice(2 * u * P, 2 * (u + 1) * P)
-                nc.vector.quantize_mx(out=w_codes[i][:, cols].bitcast(FP8X4), scales=w_scales[i][:, cols], in_=w_bf[i][:, 2 * u : 2 * u + 2].rearrange("p t m r -> p (t m r)"))
+        def quantise_weights(i, calls):
+            for t0, t1 in calls:
+                cols = slice(t0 * P, t1 * P)
+                nc.vector.quantize_mx(out=w_codes[i][:, cols].bitcast(FP8X4), scales=w_scales[i][:, cols], in_=w_bf[i][:, t0:t1].rearrange("p t m r -> p (t m r)"))
 
 
         def product(bank_part, i, t, tokens):
@@ -118,24 +121,25 @@ def tile_picked_maxout_max_lo_kernel(tc, xT, w1, w2, w3, offs, out_0, out_1, out
             nc.vector.tensor_tensor(part, bank, part, mybir.AluOpType.max)
 
         round_weights(0, [("scalar", 0, 56), ("vector", 56, 128)], "w_bf0")
-        quantise_weights(0)
+        quantise_weights(0, ((0, 1), (1, 2), (2, 4)))
         quantise_tokens(1, "w_raw0_0")
         banks = multiply(0, ((0, 0), (0, 1), (1, 0)))
-        round_weights(1, [("scalar", 0, 64), ("scalar", 64, 76), ("vector", 76, 128)], "w_bf1")
-        y_all = keep.tile([P, 2, PACK, HALF], F32, name="y_all", tag="w_raw1_64", align_bytes=64)
+        round_weights(1, [("scalar", 0, 64), ("vector", 64, 128)], "w_bf1")
+        y_all = keep.tile([P, 2, PACK, HALF], F32, name="y_all", tag="w_raw1_0", align_bytes=64)
         y = [y_all[:, c] for c in range(2)]
         for (c, u), bank in banks.items():
             nc.scalar.copy(out=y[c][:, 2 * u : 2 * u + 2, :], in_=bank[:])
-        quantise_weights(1)
+        quantise_weights(1, ((0, 1), (1, 2), (2, 4)))
         banks = multiply(1, ((0, 0),))
-        nc.scalar.copy(out=y[1][:, 2:4, :], in_=multiply(0, ((1, 1),))[1, 1][:])
+        late = multiply(0, ((1, 1),))[1, 1]
         banks = {**banks, **multiply(1, ((0, 1), (1, 0), (1, 1)))}
+        round_weights(2, [("vector", 0, 32), ("gpsimd", 32, 64), ("gpsimd", 64, 84), ("scalar", 84, 128)], "w_bf1")
         for (c, u) in ((0, 0), (0, 1), (1, 0)):
             take_max(y[c][:, 2 * u : 2 * u + 2, :], banks[c, u][:])
-        round_weights(2, [("gpsimd", 0, 64), ("gpsimd", 64, 92), ("scalar", 92, 128)], "w_bf1")
-        quantise_weights(2, (0,))
-        take_max(y[1][:, 2:4, :], banks[1, 1][:])
-        quantise_weights(2, (1,))
+        held = keep.tile([P, 2, HALF], F32, name="held", tag="w_raw2_64", align_bytes=64)
+        nc.scalar.copy(out=held[:], in_=late[:])
+        quantise_weights(2, ((0, 2), (2, 4)))
+        nc.vector.tensor_tensor(y[1][:, 2:4, :], banks[1, 1][:], held[:], mybir.AluOpType.max)
 
         y_rows = out_0.rearrange("(p t) s -> p t s", t=PACK)
         y_codes = keep.tile([P, S], U32, name="y_codes", align_bytes=64)
@@ -143,32 +147,27 @@ def tile_picked_maxout_max_lo_kernel(tc, xT, w1, w2, w3, offs, out_0, out_1, out
         y_bf = [keep.tile([P, width, PACK], BF16, name=f"y_bf{g}", align_bytes=64) for g, width in enumerate((HALF, P, P))]
         words = out_1[0].rearrange("p s r -> p (s r)").bitcast(I32)
 
-        banks = multiply(2, ((0, 0), (0, 1)))
-        quarters = []
-        for g in range(2):
-            bank = psum.tile([P, PACK, P], F32, name=f"quarter{g}", tag=f"bank{BANKS[2][2 + g]}")
-            for t in range(PACK):
-                product(bank[:, t, :], 2, t, slice(HALF + g * P, HALF + (g + 1) * P))
-            quarters.append(bank)
-        for u in range(2):
-            part = y[0][:, 2 * u : 2 * u + 2, :]
-            take_max(part, banks[0, u][:])
-            nc.sync.dma_start(y_rows[:, 2 * u : 2 * u + 2, 0:HALF], part)
-        interleave(nc, "scalar", y_bf[0][:], y[0])
-        for g in range(2):
-            part = y[1][:, :, g * P : (g + 1) * P]
-            take_max(part, quarters[g][:])
-            nc.sync.dma_start(y_rows[:, :, HALF + g * P : HALF + (g + 1) * P], part)
-        interleave(nc, "scalar", y_bf[1][:], y[1][:, :, 0:P])
-        interleave(nc, "vector", y_bf[2][:], y[1][:, :, P:HALF])
+        def store_rows(c, u):
+            nc.sync.dma_start(y_rows[:, 2 * u : 2 * u + 2, c * HALF : (c + 1) * HALF], y[c][:, 2 * u : 2 * u + 2, :])
 
         def quantise_result(g, cols):
             nc.vector.quantize_mx(out=y_codes[:, cols].bitcast(FP8X4), scales=y_scales[:, cols], in_=y_bf[g][:].rearrange("p c r -> p (c r)"))
 
+        banks = multiply(2, ((0, 0), (0, 1), (1, 0), (1, 1)))
+        for c, u in ((0, 0), (0, 1), (1, 0)):
+            take_max(y[c][:, 2 * u : 2 * u + 2, :], banks[c, u][:])
+            store_rows(c, u)
+        interleave(nc, "scalar", y_bf[0][:, 0:P, :], y[0][:, :, 0:P])
+        interleave(nc, "gpsimd", y_bf[0][:, P:HALF, :], y[0][:, :, P:HALF])
+        for g in range(2):
+            take_max(y[1][:, 2:4, g * P : (g + 1) * P], banks[1, 1][:, :, g * P : (g + 1) * P])
+        store_rows(1, 1)
+        interleave(nc, "scalar", y_bf[1][:], y[1][:, :, 0:P])
         quantise_result(0, slice(0, HALF))
         nc.sync.dma_start(words[:, 0:HALF], y_codes[:, 0:HALF].bitcast(I32))
-        quantise_result(2, slice(HALF + P, S))
+        interleave(nc, "vector", y_bf[2][:], y[1][:, :, P:HALF])
         quantise_result(1, slice(HALF, HALF + P))
+        quantise_result(2, slice(HALF + P, S))
         nc.sync.dma_start(words[:, HALF:S], y_codes[:, HALF:S].bitcast(I32))
         for q in range(4):
             queue = nc.scalar if q % 2 == 0 else nc.sync

@@ -12,11 +12,23 @@ U32 = mybir.dt.uint32
 U16 = mybir.dt.uint16
 U8 = mybir.dt.uint8
 FP8X4 = mybir.dt.float8_e4m3fn_x4
+MAX = mybir.AluOpType.max
 
 P = 128
 PACK = 4
-HALF = 256
-LOADS = (((0, 128),), ((0, 64), (64, 128)), ((0, 64), (64, 128)))
+HALF = S // 2
+QUARTER = S // 4
+LIST_ROWS = 16
+
+W2_CUT = 96
+W3_CUT = 64
+LOADS = (((0, P),), ((0, W2_CUT), (W2_CUT, P)), ((0, W3_CUT), (W3_CUT, P)))
+
+W1_SCALAR = 48
+W2_SCALAR = 60
+W3_VECTOR = 16
+W3_GPSIMD_END = 84
+
 BANKS = ((0, 1, 2, 0), (3, 4, 5, 6), (7, 1, 2, 3))
 
 
@@ -32,12 +44,12 @@ def copy_on(nc, engine, out, in_):
 def interleave(nc, engine, grouped, planes):
     if engine == "gpsimd":
         copy_on(nc, engine, grouped, planes.rearrange("p r c -> p c r"))
-        return
-    copy_on(
-        nc, engine,
-        grouped.rearrange("p (c i) r -> p c r i", i=4),
-        planes.rearrange("p r (c i) -> p c r i", i=4),
-    )
+    else:
+        copy_on(
+            nc, engine,
+            grouped.rearrange("p (c i) r -> p c r i", i=4),
+            planes.rearrange("p r (c i) -> p c r i", i=4),
+        )
 
 
 def tile_picked_maxout_max_lo_kernel(tc, xT, w1, w2, w3, offs, out_0, out_1, out_2):
@@ -47,7 +59,7 @@ def tile_picked_maxout_max_lo_kernel(tc, xT, w1, w2, w3, offs, out_0, out_1, out
         psum = ctx.enter_context(tc.psum_pool(name="psum", bufs=1))
 
         x_rows = xT.rearrange("(p r) t -> p r t", r=PACK)
-        offsets = keep.tile([P, S // 16], U16, name="offsets")
+        offsets = keep.tile([P, S // LIST_ROWS], U16, name="offsets")
         x_raw = [keep.tile([P, T], F32, name=f"x_raw{r}") for r in range(PACK)]
         nc.sync.dma_start(x_raw[0][:], x_rows[:, 0, :])
         nc.sync.dma_start(offsets[:], offs)
@@ -62,19 +74,24 @@ def tile_picked_maxout_max_lo_kernel(tc, xT, w1, w2, w3, offs, out_0, out_1, out
         picked = keep.tile([P, PACK, S], F32, name="picked")
         for r in range(PACK - 1):
             nc.vector.tensor_copy(picked[:, r, :], x_raw[r][:].indirect(offsets[:]))
-        for g in range(4):
-            nc.vector.tensor_copy(picked[:, PACK - 1, g * 128 : (g + 1) * 128], x_raw[PACK - 1][:].indirect(offsets[:, g * 8 : (g + 1) * 8]))
+        quarters = [slice(g * QUARTER, (g + 1) * QUARTER) for g in range(4)]
+        for tokens in quarters:
+            entries = offsets[:, tokens.start // LIST_ROWS : tokens.stop // LIST_ROWS]
+            nc.vector.tensor_copy(picked[:, PACK - 1, tokens], x_raw[PACK - 1][:].indirect(entries))
 
         x_codes = {}
         x_scales = keep.tile([P, S], U8, name="x_scales", align_bytes=64)
         x_bf = keep.tile([P, S, PACK], BF16, name="x_bf", align_bytes=64)
-        for g, engine in enumerate(("scalar", "scalar", "vector", "vector")):
-            interleave(nc, engine, x_bf[:, g * 128 : (g + 1) * 128, :], picked[:, :, g * 128 : (g + 1) * 128])
+        for tokens, engine in zip(quarters, ("scalar", "scalar", "vector", "vector")):
+            interleave(nc, engine, x_bf[:, tokens, :], picked[:, :, tokens])
 
         def quantise_tokens(c, tag):
-            cols = slice(c * HALF, (c + 1) * HALF)
+            tokens = slice(c * HALF, (c + 1) * HALF)
             x_codes[c] = keep.tile([P, HALF], U32, name=f"x_codes{c}", tag=tag, align_bytes=64)
-            nc.vector.quantize_mx(out=x_codes[c][:].bitcast(FP8X4), scales=x_scales[:, cols], in_=x_bf[:, cols, :].rearrange("p c r -> p (c r)"))
+            nc.vector.quantize_mx(
+                out=x_codes[c][:].bitcast(FP8X4), scales=x_scales[:, tokens],
+                in_=x_bf[:, tokens, :].rearrange("p c r -> p (c r)"),
+            )
 
         quantise_tokens(0, "x_codes0")
 
@@ -85,90 +102,105 @@ def tile_picked_maxout_max_lo_kernel(tc, xT, w1, w2, w3, offs, out_0, out_1, out
         def round_weights(i, shares, tag):
             w_bf[i] = keep.tile([P, PACK, P, PACK], BF16, name=f"w_bf{i}", tag=tag, align_bytes=64)
             for engine, m0, m1 in shares:
-                first = max(a for a, b in LOADS[i] if a <= m0)
+                first = max(start for start, stop in LOADS[i] if start <= m0)
+                walk = "p m t r" if engine == "gpsimd" else "p m r t"
                 copy_on(
                     nc, engine,
-                    w_bf[i][:, :, m0:m1, :].rearrange("p t m r -> p m t r" if engine == "gpsimd" else "p t m r -> p m r t"),
-                    w_raw[i, first][:, :, PACK * (m0 - first) : PACK * (m1 - first)].rearrange("p r (m t) -> p m t r" if engine == "gpsimd" else "p r (m t) -> p m r t", t=PACK),
+                    w_bf[i][:, :, m0:m1, :].rearrange(f"p t m r -> {walk}"),
+                    w_raw[i, first][:, :, PACK * (m0 - first) : PACK * (m1 - first)].rearrange(f"p r (m t) -> {walk}", t=PACK),
                 )
 
         def quantise_weights(i, calls):
             for t0, t1 in calls:
                 cols = slice(t0 * P, t1 * P)
-                nc.vector.quantize_mx(out=w_codes[i][:, cols].bitcast(FP8X4), scales=w_scales[i][:, cols], in_=w_bf[i][:, t0:t1].rearrange("p t m r -> p (t m r)"))
+                nc.vector.quantize_mx(
+                    out=w_codes[i][:, cols].bitcast(FP8X4), scales=w_scales[i][:, cols],
+                    in_=w_bf[i][:, t0:t1].rearrange("p t m r -> p (t m r)"),
+                )
 
+        def multiply(i, c, u):
+            bank = psum.tile([P, 2, HALF], F32, name=f"bank{i}{c}{u}", tag=f"bank{BANKS[i][2 * c + u]}")
+            for e in range(2):
+                cols = slice((2 * u + e) * P, (2 * u + e + 1) * P)
+                nc.tensor.matmul_mx(
+                    out=bank[:, e, :],
+                    lhsT=w_codes[i][:, cols].bitcast(FP8X4),
+                    lhsT_scale=w_scales[i][:, cols],
+                    rhs=x_codes[c][:].bitcast(FP8X4),
+                    rhs_scale=x_scales[:, c * HALF : (c + 1) * HALF],
+                    start=True, stop=True,
+                )
+            return bank
 
-        def product(bank_part, i, t, tokens):
-            nc.tensor.matmul_mx(
-                out=bank_part,
-                lhsT=w_codes[i][:, t * P : (t + 1) * P].bitcast(FP8X4),
-                lhsT_scale=w_scales[i][:, t * P : (t + 1) * P],
-                rhs=x_codes[tokens.start // HALF][:, tokens.start % HALF : (tokens.stop - 1) % HALF + 1].bitcast(FP8X4),
-                rhs_scale=x_scales[:, tokens],
-                start=True, stop=True,
-            )
+        first_tiles_singly = ((0, 1), (1, 2), (2, 4))
+        leading = ((0, 0), (0, 1), (1, 0))
 
-        def multiply(i, parts):
-            banks = {}
-            for c, u in parts:
-                if True:
-                    banks[c, u] = psum.tile([P, 2, HALF], F32, name=f"bank{i}{c}{u}", tag=f"bank{BANKS[i][2 * c + u]}")
-                    for e in range(2):
-                        product(banks[c, u][:, e, :], i, 2 * u + e, slice(c * HALF, (c + 1) * HALF))
-            return banks
-
-        def take_max(part, bank):
-            nc.vector.tensor_tensor(part, bank, part, mybir.AluOpType.max)
-
-        round_weights(0, [("scalar", 0, 56), ("vector", 56, 128)], "w_bf0")
-        quantise_weights(0, ((0, 1), (1, 2), (2, 4)))
+        round_weights(0, [("scalar", 0, W1_SCALAR), ("vector", W1_SCALAR, P)], "w_bf0")
+        quantise_weights(0, first_tiles_singly)
         quantise_tokens(1, "w_raw0_0")
-        banks = multiply(0, ((0, 0), (0, 1), (1, 0)))
-        round_weights(1, [("scalar", 0, 64), ("vector", 64, 128)], "w_bf1")
+        w1_banks = {part: multiply(0, *part) for part in leading}
+
+        round_weights(1, [("scalar", 0, W2_SCALAR), ("vector", W2_SCALAR, W2_CUT), ("vector", W2_CUT, P)], "w_bf1")
         y_all = keep.tile([P, 2, PACK, HALF], F32, name="y_all", tag="w_raw1_0", align_bytes=64)
         y = [y_all[:, c] for c in range(2)]
-        for (c, u), bank in banks.items():
-            nc.scalar.copy(out=y[c][:, 2 * u : 2 * u + 2, :], in_=bank[:])
-        quantise_weights(1, ((0, 1), (1, 2), (2, 4)))
-        banks = multiply(1, ((0, 0),))
-        late = multiply(0, ((1, 1),))[1, 1]
-        banks = {**banks, **multiply(1, ((0, 1), (1, 0), (1, 1)))}
-        round_weights(2, [("vector", 0, 32), ("gpsimd", 32, 64), ("gpsimd", 64, 84), ("scalar", 84, 128)], "w_bf1")
-        for (c, u) in ((0, 0), (0, 1), (1, 0)):
-            take_max(y[c][:, 2 * u : 2 * u + 2, :], banks[c, u][:])
-        held = keep.tile([P, 2, HALF], F32, name="held", tag="w_raw2_64", align_bytes=64)
-        nc.scalar.copy(out=held[:], in_=late[:])
+
+        def pair(c, u):
+            return y[c][:, 2 * u : 2 * u + 2, :]
+
+        for part in leading:
+            nc.scalar.copy(out=pair(*part), in_=w1_banks[part][:])
+        quantise_weights(1, first_tiles_singly)
+        w2_banks = {(0, 0): multiply(1, 0, 0)}
+        w1_last = multiply(0, 1, 1)
+        for part in ((0, 1), (1, 0), (1, 1)):
+            w2_banks[part] = multiply(1, *part)
+
+        round_weights(
+            2,
+            [("vector", 0, W3_VECTOR), ("gpsimd", W3_VECTOR, W3_CUT), ("gpsimd", W3_CUT, W3_GPSIMD_END), ("scalar", W3_GPSIMD_END, P)],
+            "w_bf1",
+        )
+        for part in leading:
+            nc.vector.tensor_tensor(pair(*part), w2_banks[part][:], pair(*part), MAX)
+
+        held = keep.tile([P, 2, HALF], F32, name="held", tag=f"w_raw2_{W3_CUT}", align_bytes=64)
+        nc.scalar.copy(out=held[:], in_=w1_last[:])
         quantise_weights(2, ((0, 2), (2, 4)))
-        nc.vector.tensor_tensor(y[1][:, 2:4, :], banks[1, 1][:], held[:], mybir.AluOpType.max)
+        nc.vector.tensor_tensor(pair(1, 1), w2_banks[1, 1][:], held[:], MAX)
 
         y_rows = out_0.rearrange("(p t) s -> p t s", t=PACK)
         y_codes = keep.tile([P, S], U32, name="y_codes", align_bytes=64)
         y_scales = keep.tile([P, S], U8, name="y_scales", align_bytes=64)
-        y_bf = [keep.tile([P, width, PACK], BF16, name=f"y_bf{g}", align_bytes=64) for g, width in enumerate((HALF, P, P))]
+        pieces = (slice(0, HALF), quarters[2], quarters[3])
+        y_bf = [keep.tile([P, tokens.stop - tokens.start, PACK], BF16, name=f"y_bf{g}", align_bytes=64) for g, tokens in enumerate(pieces)]
         words = out_1[0].rearrange("p s r -> p (s r)").bitcast(I32)
 
         def store_rows(c, u):
-            nc.sync.dma_start(y_rows[:, 2 * u : 2 * u + 2, c * HALF : (c + 1) * HALF], y[c][:, 2 * u : 2 * u + 2, :])
+            nc.sync.dma_start(y_rows[:, 2 * u : 2 * u + 2, c * HALF : (c + 1) * HALF], pair(c, u))
 
-        def quantise_result(g, cols):
-            nc.vector.quantize_mx(out=y_codes[:, cols].bitcast(FP8X4), scales=y_scales[:, cols], in_=y_bf[g][:].rearrange("p c r -> p (c r)"))
+        def quantise_result(g):
+            nc.vector.quantize_mx(
+                out=y_codes[:, pieces[g]].bitcast(FP8X4), scales=y_scales[:, pieces[g]],
+                in_=y_bf[g][:].rearrange("p c r -> p (c r)"),
+            )
 
-        banks = multiply(2, ((0, 0), (0, 1), (1, 0), (1, 1)))
-        for c, u in ((0, 0), (0, 1), (1, 0)):
-            take_max(y[c][:, 2 * u : 2 * u + 2, :], banks[c, u][:])
-            store_rows(c, u)
-        interleave(nc, "scalar", y_bf[0][:, 0:P, :], y[0][:, :, 0:P])
-        interleave(nc, "gpsimd", y_bf[0][:, P:HALF, :], y[0][:, :, P:HALF])
-        for g in range(2):
-            take_max(y[1][:, 2:4, g * P : (g + 1) * P], banks[1, 1][:, :, g * P : (g + 1) * P])
+        w3_banks = {part: multiply(2, *part) for part in leading + ((1, 1),)}
+        for part in leading:
+            nc.vector.tensor_tensor(pair(*part), w3_banks[part][:], pair(*part), MAX)
+            store_rows(*part)
+        interleave(nc, "scalar", y_bf[0][:, quarters[0], :], y[0][:, :, quarters[0]])
+        interleave(nc, "gpsimd", y_bf[0][:, quarters[1], :], y[0][:, :, quarters[1]])
+        for tokens in quarters[:2]:
+            nc.vector.tensor_tensor(pair(1, 1)[:, :, tokens], w3_banks[1, 1][:, :, tokens], pair(1, 1)[:, :, tokens], MAX)
         store_rows(1, 1)
-        interleave(nc, "scalar", y_bf[1][:], y[1][:, :, 0:P])
-        quantise_result(0, slice(0, HALF))
+        interleave(nc, "scalar", y_bf[1][:], y[1][:, :, quarters[0]])
+        quantise_result(0)
         nc.sync.dma_start(words[:, 0:HALF], y_codes[:, 0:HALF].bitcast(I32))
-        interleave(nc, "vector", y_bf[2][:], y[1][:, :, P:HALF])
-        quantise_result(1, slice(HALF, HALF + P))
-        quantise_result(2, slice(HALF + P, S))
+        interleave(nc, "vector", y_bf[2][:], y[1][:, :, quarters[1]])
+        quantise_result(1)
+        quantise_result(2)
         nc.sync.dma_start(words[:, HALF:S], y_codes[:, HALF:S].bitcast(I32))
-        for q in range(4):
-            queue = nc.scalar if q % 2 == 0 else nc.sync
-            queue.dma_start(out_2[0, 4 * q : 4 * q + 4, :].bitcast(I32), y_scales[32 * q : 32 * q + 4, :].bitcast(I32))
+
+        for Q in range(4):
+            queue = nc.scalar if Q % 2 == 0 else nc.sync
+            queue.dma_start(out_2[0, 4 * Q : 4 * Q + 4, :].bitcast(I32), y_scales[32 * Q : 32 * Q + 4, :].bitcast(I32))

@@ -20,20 +20,27 @@ HALF = S // 2
 QUARTER = S // 4
 LIST_ROWS = 16
 
-W2_CUT = 96
+W2_CUTS = (0, 64, 96, P)
 W3_CUT = 64
-LOADS = (((0, P),), ((0, W2_CUT), (W2_CUT, P)), ((0, W3_CUT), (W3_CUT, P)))
+W1_CUT = 96
+LOADS = (((0, W1_CUT), (W1_CUT, P)), tuple(zip(W2_CUTS, W2_CUTS[1:])), ((0, W3_CUT), (W3_CUT, P)))
 
 W1_SCALAR = 48
-W2_SCALAR = 60
-W3_VECTOR = 16
-W3_GPSIMD_END = 84
+FIRST_ROW_SCALAR = 64
+X_SCALAR = 160
+W2_SCALAR = 48
+W3_VECTOR = 24
+W3_GPSIMD_END = 94
 
-BANKS = ((0, 1, 2, 0), (3, 4, 5, 6), (7, 1, 2, 3))
+BANKS = ((0, 1, 2, 1), (3, 4, 5, 2), (0, 6, 7, 3))
 
 
-def copy_on(nc, engine, out, in_):
-    if engine == "scalar":
+def copy_on(nc, engine, out, in_, negate=False):
+    if negate and engine == "scalar":
+        nc.scalar.mul(out, in_, -1.0)
+    elif negate:
+        nc.vector.tensor_scalar_mul(out, in_, -1.0)
+    elif engine == "scalar":
         nc.scalar.copy(out=out, in_=in_)
     elif engine == "vector":
         nc.vector.tensor_copy(out=out, in_=in_)
@@ -61,29 +68,40 @@ def tile_picked_maxout_max_lo_kernel(tc, xT, w1, w2, w3, offs, out_0, out_1, out
         x_rows = xT.rearrange("(p r) t -> p r t", r=PACK)
         offsets = keep.tile([P, S // LIST_ROWS], U16, name="offsets")
         x_raw = [keep.tile([P, T], F32, name=f"x_raw{r}") for r in range(PACK)]
+        w_raw = {}
+
+        def load_weights(i, part):
+            m0, m1 = LOADS[i][part]
+            w_raw[i, m0] = keep.tile([P, PACK, PACK * (m1 - m0)], F32, name=f"w_raw{i}_{m0}", tag=f"w_raw{i}_{m0}", align_bytes=64)
+            nc.sync.dma_start(w_raw[i, m0][:], (w1, w2, w3)[i].rearrange("(p r) n -> p r n", r=PACK)[:, :, PACK * m0 : PACK * m1])
+
         nc.sync.dma_start(x_raw[0][:], x_rows[:, 0, :])
         nc.sync.dma_start(offsets[:], offs)
         for r in range(1, PACK):
             nc.sync.dma_start(x_raw[r][:], x_rows[:, r, :])
-        w_raw = {}
-        for i, w in enumerate((w1, w2, w3)):
-            for m0, m1 in LOADS[i]:
-                w_raw[i, m0] = keep.tile([P, PACK, PACK * (m1 - m0)], F32, name=f"w_raw{i}_{m0}", tag=f"w_raw{i}_{m0}", align_bytes=64)
-                nc.sync.dma_start(w_raw[i, m0][:], w.rearrange("(p r) n -> p r n", r=PACK)[:, :, PACK * m0 : PACK * m1])
+        for i in range(3):
+            for part in range(len(LOADS[i])):
+                load_weights(i, part)
 
-        picked = keep.tile([P, PACK, S], F32, name="picked")
-        for r in range(PACK - 1):
-            nc.vector.tensor_copy(picked[:, r, :], x_raw[r][:].indirect(offsets[:]))
+        picked = [keep.tile([P, PACK, HALF], F32, name=f"picked{c}") for c in range(2)]
+
+        def window(r, j0, j1):
+            return x_raw[r][:].indirect(offsets[:, j0 // LIST_ROWS : j1 // LIST_ROWS])
+
+        for r in range(PACK):
+            nc.vector.tensor_copy(picked[0][:, r, :], window(r, 0, HALF))
+            share = FIRST_ROW_SCALAR if r == 0 else HALF
+            nc.scalar.activation(picked[1][:, r, HALF - share :], window(r, S - share, S), mybir.ActivationFunctionType.Copy)
+            if share < HALF:
+                nc.vector.tensor_copy(picked[1][:, r, : HALF - share], window(r, HALF, S - share))
         quarters = [slice(g * QUARTER, (g + 1) * QUARTER) for g in range(4)]
-        for tokens in quarters:
-            entries = offsets[:, tokens.start // LIST_ROWS : tokens.stop // LIST_ROWS]
-            nc.vector.tensor_copy(picked[:, PACK - 1, tokens], x_raw[PACK - 1][:].indirect(entries))
 
         x_codes = {}
         x_scales = keep.tile([P, S], U8, name="x_scales", align_bytes=64)
         x_bf = keep.tile([P, S, PACK], BF16, name="x_bf", align_bytes=64)
-        for tokens, engine in zip(quarters, ("scalar", "scalar", "vector", "vector")):
-            interleave(nc, engine, x_bf[:, tokens, :], picked[:, :, tokens])
+        interleave(nc, "vector", x_bf[:, 0:HALF, :], picked[0][:])
+        interleave(nc, "vector", x_bf[:, HALF : S - X_SCALAR, :], picked[1][:, :, : HALF - X_SCALAR])
+        interleave(nc, "scalar", x_bf[:, S - X_SCALAR :, :], picked[1][:, :, HALF - X_SCALAR :])
 
         def quantise_tokens(c, tag):
             tokens = slice(c * HALF, (c + 1) * HALF)
@@ -108,6 +126,7 @@ def tile_picked_maxout_max_lo_kernel(tc, xT, w1, w2, w3, offs, out_0, out_1, out
                     nc, engine,
                     w_bf[i][:, :, m0:m1, :].rearrange(f"p t m r -> {walk}"),
                     w_raw[i, first][:, :, PACK * (m0 - first) : PACK * (m1 - first)].rearrange(f"p r (m t) -> {walk}", t=PACK),
+                    negate=(i == 1),
                 )
 
         def quantise_weights(i, calls):
@@ -118,29 +137,32 @@ def tile_picked_maxout_max_lo_kernel(tc, xT, w1, w2, w3, offs, out_0, out_1, out
                     in_=w_bf[i][:, t0:t1].rearrange("p t m r -> p (t m r)"),
                 )
 
-        def multiply(i, c, u):
+        def multiply(i, c, u, also=()):
             bank = psum.tile([P, 2, HALF], F32, name=f"bank{i}{c}{u}", tag=f"bank{BANKS[i][2 * c + u]}")
             for e in range(2):
                 cols = slice((2 * u + e) * P, (2 * u + e + 1) * P)
-                nc.tensor.matmul_mx(
-                    out=bank[:, e, :],
-                    lhsT=w_codes[i][:, cols].bitcast(FP8X4),
-                    lhsT_scale=w_scales[i][:, cols],
-                    rhs=x_codes[c][:].bitcast(FP8X4),
-                    rhs_scale=x_scales[:, c * HALF : (c + 1) * HALF],
-                    start=True, stop=True,
-                )
+                terms = (i,) + also
+                for j in terms:
+                    nc.tensor.matmul_mx(
+                        out=bank[:, e, :],
+                        lhsT=w_codes[j][:, cols].bitcast(FP8X4),
+                        lhsT_scale=w_scales[j][:, cols],
+                        rhs=x_codes[c][:].bitcast(FP8X4),
+                        rhs_scale=x_scales[:, c * HALF : (c + 1) * HALF],
+                        start=(j == terms[0]), stop=(j == terms[-1]),
+                    )
             return bank
 
         first_tiles_singly = ((0, 1), (1, 2), (2, 4))
         leading = ((0, 0), (0, 1), (1, 0))
 
-        round_weights(0, [("scalar", 0, W1_SCALAR), ("vector", W1_SCALAR, P)], "w_bf0")
-        quantise_weights(0, first_tiles_singly)
-        quantise_tokens(1, "w_raw0_0")
+        round_weights(0, [("scalar", 0, W1_SCALAR), ("vector", W1_SCALAR, W1_CUT), ("vector", W1_CUT, P)], "w_bf0")
+        quantise_weights(0, first_tiles_singly[:2])
+        quantise_tokens(1, f"w_raw0_{W1_CUT}")
+        quantise_weights(0, first_tiles_singly[2:])
         w1_banks = {part: multiply(0, *part) for part in leading}
 
-        round_weights(1, [("scalar", 0, W2_SCALAR), ("vector", W2_SCALAR, W2_CUT), ("vector", W2_CUT, P)], "w_bf1")
+        round_weights(1, [("scalar", 0, W2_SCALAR), ("vector", W2_SCALAR, W2_CUTS[1]), ("vector", W2_CUTS[1], W2_CUTS[2]), ("vector", W2_CUTS[2], P)], "w_bf1")
         y_all = keep.tile([P, 2, PACK, HALF], F32, name="y_all", tag="w_raw1_0", align_bytes=64)
         y = [y_all[:, c] for c in range(2)]
 
@@ -150,10 +172,9 @@ def tile_picked_maxout_max_lo_kernel(tc, xT, w1, w2, w3, offs, out_0, out_1, out
         for part in leading:
             nc.scalar.copy(out=pair(*part), in_=w1_banks[part][:])
         quantise_weights(1, first_tiles_singly)
-        w2_banks = {(0, 0): multiply(1, 0, 0)}
+        w2_banks = {part: multiply(1, *part) for part in leading}
         w1_last = multiply(0, 1, 1)
-        for part in ((0, 1), (1, 0), (1, 1)):
-            w2_banks[part] = multiply(1, *part)
+        difference = multiply(1, 1, 1, also=(0,))
 
         round_weights(
             2,
@@ -161,12 +182,15 @@ def tile_picked_maxout_max_lo_kernel(tc, xT, w1, w2, w3, offs, out_0, out_1, out
             "w_bf1",
         )
         for part in leading:
-            nc.vector.tensor_tensor(pair(*part), w2_banks[part][:], pair(*part), MAX)
+            nc.vector.scalar_tensor_tensor(pair(*part), w2_banks[part][:], -1.0, pair(*part), mybir.AluOpType.mult, MAX)
 
-        held = keep.tile([P, 2, HALF], F32, name="held", tag=f"w_raw2_{W3_CUT}", align_bytes=64)
-        nc.scalar.copy(out=held[:], in_=w1_last[:])
+        terms = keep.tile([P, 2, 2, HALF], F32, name="terms", tag=f"w_raw2_{W3_CUT}", align_bytes=64)
+        held, excess = terms[:, 0], terms[:, 1]
+        nc.scalar.copy(out=held, in_=w1_last[:])
+        nc.scalar.activation(excess, difference[:], mybir.ActivationFunctionType.Relu, scale=-1.0)
         quantise_weights(2, ((0, 2), (2, 4)))
-        nc.vector.tensor_tensor(pair(1, 1), w2_banks[1, 1][:], held[:], MAX)
+        last_max = keep.tile([P, 2, HALF], F32, name="last_max", tag="w_bf1", align_bytes=64)
+        nc.gpsimd.tensor_tensor(last_max[:], held, excess, mybir.AluOpType.add)
 
         y_rows = out_0.rearrange("(p t) s -> p t s", t=PACK)
         y_codes = keep.tile([P, S], U32, name="y_codes", align_bytes=64)
@@ -191,7 +215,7 @@ def tile_picked_maxout_max_lo_kernel(tc, xT, w1, w2, w3, offs, out_0, out_1, out
         interleave(nc, "scalar", y_bf[0][:, quarters[0], :], y[0][:, :, quarters[0]])
         interleave(nc, "gpsimd", y_bf[0][:, quarters[1], :], y[0][:, :, quarters[1]])
         for tokens in quarters[:2]:
-            nc.vector.tensor_tensor(pair(1, 1)[:, :, tokens], w3_banks[1, 1][:, :, tokens], pair(1, 1)[:, :, tokens], MAX)
+            nc.vector.tensor_tensor(pair(1, 1)[:, :, tokens], w3_banks[1, 1][:, :, tokens], last_max[:, :, tokens], MAX)
         store_rows(1, 1)
         interleave(nc, "scalar", y_bf[1][:], y[1][:, :, quarters[0]])
         quantise_result(0)

@@ -21,16 +21,12 @@ QUARTER = S // 4
 LIST_ROWS = 16
 
 W2_CUTS = (0, 64, 96, P)
-W3_CUT = 64
-W1_CUT = 96
-LOADS = (((0, W1_CUT), (W1_CUT, P)), tuple(zip(W2_CUTS, W2_CUTS[1:])), ((0, W3_CUT), (W3_CUT, P)))
+W3_CUTS = (0, 64, 96, P)
+LOADS = (((0, P),), tuple(zip(W2_CUTS, W2_CUTS[1:])), tuple(zip(W3_CUTS, W3_CUTS[1:])))
 
 W1_SCALAR = 48
-FIRST_ROW_SCALAR = 64
-X_SCALAR = 160
-W2_SCALAR = 48
-W3_VECTOR = 24
-W3_GPSIMD_END = 94
+W2_SHARED = 112
+W3_GPSIMD_END = 110
 
 BANKS = ((0, 1, 2, 1), (3, 4, 5, 2), (0, 6, 7, 3))
 
@@ -83,25 +79,19 @@ def tile_picked_maxout_max_lo_kernel(tc, xT, w1, w2, w3, offs, out_0, out_1, out
             for part in range(len(LOADS[i])):
                 load_weights(i, part)
 
-        picked = [keep.tile([P, PACK, HALF], F32, name=f"picked{c}") for c in range(2)]
-
-        def window(r, j0, j1):
-            return x_raw[r][:].indirect(offsets[:, j0 // LIST_ROWS : j1 // LIST_ROWS])
-
-        for r in range(PACK):
-            nc.vector.tensor_copy(picked[0][:, r, :], window(r, 0, HALF))
-            share = FIRST_ROW_SCALAR if r == 0 else HALF
-            nc.scalar.activation(picked[1][:, r, HALF - share :], window(r, S - share, S), mybir.ActivationFunctionType.Copy)
-            if share < HALF:
-                nc.vector.tensor_copy(picked[1][:, r, : HALF - share], window(r, HALF, S - share))
+        picked = keep.tile([P, PACK, S], F32, name="picked")
+        for r in range(PACK - 1):
+            nc.vector.tensor_copy(picked[:, r, :], x_raw[r][:].indirect(offsets[:]))
         quarters = [slice(g * QUARTER, (g + 1) * QUARTER) for g in range(4)]
+        for tokens in quarters:
+            entries = offsets[:, tokens.start // LIST_ROWS : tokens.stop // LIST_ROWS]
+            nc.vector.tensor_copy(picked[:, PACK - 1, tokens], x_raw[PACK - 1][:].indirect(entries))
 
         x_codes = {}
         x_scales = keep.tile([P, S], U8, name="x_scales", align_bytes=64)
         x_bf = keep.tile([P, S, PACK], BF16, name="x_bf", align_bytes=64)
-        interleave(nc, "vector", x_bf[:, 0:HALF, :], picked[0][:])
-        interleave(nc, "vector", x_bf[:, HALF : S - X_SCALAR, :], picked[1][:, :, : HALF - X_SCALAR])
-        interleave(nc, "scalar", x_bf[:, S - X_SCALAR :, :], picked[1][:, :, HALF - X_SCALAR :])
+        for tokens, engine in zip(quarters, ("scalar", "scalar", "vector", "vector")):
+            interleave(nc, engine, x_bf[:, tokens, :], picked[:, :, tokens])
 
         def quantise_tokens(c, tag):
             tokens = slice(c * HALF, (c + 1) * HALF)
@@ -156,14 +146,13 @@ def tile_picked_maxout_max_lo_kernel(tc, xT, w1, w2, w3, offs, out_0, out_1, out
         first_tiles_singly = ((0, 1), (1, 2), (2, 4))
         leading = ((0, 0), (0, 1), (1, 0))
 
-        round_weights(0, [("scalar", 0, W1_SCALAR), ("vector", W1_SCALAR, W1_CUT), ("vector", W1_CUT, P)], "w_bf0")
-        quantise_weights(0, first_tiles_singly[:2])
-        quantise_tokens(1, f"w_raw0_{W1_CUT}")
-        quantise_weights(0, first_tiles_singly[2:])
+        round_weights(0, [("scalar", 0, W1_SCALAR), ("vector", W1_SCALAR, P)], "w_bf0")
+        quantise_weights(0, first_tiles_singly)
+        quantise_tokens(1, "w_raw0_0")
         w1_banks = {part: multiply(0, *part) for part in leading}
 
-        round_weights(1, [("scalar", 0, W2_SCALAR), ("vector", W2_SCALAR, W2_CUTS[1]), ("vector", W2_CUTS[1], W2_CUTS[2]), ("vector", W2_CUTS[2], P)], "w_bf1")
-        y_all = keep.tile([P, 2, PACK, HALF], F32, name="y_all", tag="w_raw1_0", align_bytes=64)
+        round_weights(1, [("scalar", 0, W2_CUTS[1]), ("vector", W2_CUTS[1], W2_CUTS[2]), ("vector", W2_CUTS[2], W2_SHARED), ("scalar", W2_SHARED, P)], "w_bf1")
+        y_all = keep.tile([P, 2, PACK, HALF], F32, name="y_all", tag=f"w_raw1_{W2_CUTS[2]}", align_bytes=64)
         y = [y_all[:, c] for c in range(2)]
 
         def pair(c, u):
@@ -178,13 +167,13 @@ def tile_picked_maxout_max_lo_kernel(tc, xT, w1, w2, w3, offs, out_0, out_1, out
 
         round_weights(
             2,
-            [("vector", 0, W3_VECTOR), ("gpsimd", W3_VECTOR, W3_CUT), ("gpsimd", W3_CUT, W3_GPSIMD_END), ("scalar", W3_GPSIMD_END, P)],
+            [("gpsimd", 0, W3_CUTS[1]), ("scalar", W3_CUTS[1], W3_CUTS[2]), ("gpsimd", W3_CUTS[2], W3_GPSIMD_END), ("scalar", W3_GPSIMD_END, P)],
             "w_bf1",
         )
         for part in leading:
             nc.vector.scalar_tensor_tensor(pair(*part), w2_banks[part][:], -1.0, pair(*part), mybir.AluOpType.mult, MAX)
 
-        terms = keep.tile([P, 2, 2, HALF], F32, name="terms", tag=f"w_raw2_{W3_CUT}", align_bytes=64)
+        terms = keep.tile([P, 2, 2, HALF], F32, name="terms", tag=f"w_raw2_{W3_CUTS[2]}", align_bytes=64)
         held, excess = terms[:, 0], terms[:, 1]
         nc.scalar.copy(out=held, in_=w1_last[:])
         nc.scalar.activation(excess, difference[:], mybir.ActivationFunctionType.Relu, scale=-1.0)

@@ -25,8 +25,6 @@ W3_CUTS = (0, 64, 96, P)
 LOADS = (((0, P),), tuple(zip(W2_CUTS, W2_CUTS[1:])), tuple(zip(W3_CUTS, W3_CUTS[1:])))
 
 W1_SCALAR = 48
-W2_SHARED = 112
-W3_GPSIMD_END = 110
 
 BANKS = ((0, 1, 2, 1), (3, 4, 5, 2), (0, 6, 7, 3))
 
@@ -151,8 +149,8 @@ def tile_picked_maxout_max_lo_kernel(tc, xT, w1, w2, w3, offs, out_0, out_1, out
         quantise_tokens(1, "w_raw0_0")
         w1_banks = {part: multiply(0, *part) for part in leading}
 
-        round_weights(1, [("scalar", 0, W2_CUTS[1]), ("vector", W2_CUTS[1], W2_CUTS[2]), ("vector", W2_CUTS[2], W2_SHARED), ("scalar", W2_SHARED, P)], "w_bf1")
-        y_all = keep.tile([P, 2, PACK, HALF], F32, name="y_all", tag=f"w_raw1_{W2_CUTS[2]}", align_bytes=64)
+        round_weights(1, [("scalar", 0, W2_CUTS[1]), ("vector", W2_CUTS[1], W2_CUTS[2]), ("vector", W2_CUTS[2], P)], "w_bf1")
+        y_all = keep.tile([P, 2, PACK, HALF], F32, name="y_all", tag="w_raw1_0", align_bytes=64)
         y = [y_all[:, c] for c in range(2)]
 
         def pair(c, u):
@@ -167,7 +165,7 @@ def tile_picked_maxout_max_lo_kernel(tc, xT, w1, w2, w3, offs, out_0, out_1, out
 
         round_weights(
             2,
-            [("gpsimd", 0, W3_CUTS[1]), ("scalar", W3_CUTS[1], W3_CUTS[2]), ("gpsimd", W3_CUTS[2], W3_GPSIMD_END), ("scalar", W3_GPSIMD_END, P)],
+            [("gpsimd", 0, W3_CUTS[1]), ("scalar", W3_CUTS[1], W3_CUTS[2]), ("scalar", W3_CUTS[2], P)],
             "w_bf1",
         )
         for part in leading:
@@ -201,8 +199,7 @@ def tile_picked_maxout_max_lo_kernel(tc, xT, w1, w2, w3, offs, out_0, out_1, out
         for part in leading:
             nc.vector.tensor_tensor(pair(*part), w3_banks[part][:], pair(*part), MAX)
             store_rows(*part)
-        interleave(nc, "scalar", y_bf[0][:, quarters[0], :], y[0][:, :, quarters[0]])
-        interleave(nc, "gpsimd", y_bf[0][:, quarters[1], :], y[0][:, :, quarters[1]])
+        interleave(nc, "scalar", y_bf[0][:], y[0])
         for tokens in quarters[:2]:
             nc.vector.tensor_tensor(pair(1, 1)[:, :, tokens], w3_banks[1, 1][:, :, tokens], last_max[:, :, tokens], MAX)
         store_rows(1, 1)

@@ -26,7 +26,7 @@ LOADS = (((0, P),), tuple(zip(W2_CUTS, W2_CUTS[1:])), tuple(zip(W3_CUTS, W3_CUTS
 
 W1_SCALAR = 48
 
-BANKS = ((0, 1, 2, 1), (3, 4, 5, 2), (0, 6, 7, 3))
+BANKS = ((0, 1, 2, 0), (0, 1, 2, 4), (5, 6, 7, 1))
 
 
 def copy_on(nc, engine, out, in_, negate=False):
@@ -160,8 +160,8 @@ def tile_picked_maxout_max_lo_kernel(tc, xT, w1, w2, w3, offs, out_0, out_1, out
             nc.scalar.copy(out=pair(*part), in_=w1_banks[part][:])
         quantise_weights(1, first_tiles_singly)
         w2_banks = {part: multiply(1, *part) for part in leading}
-        w1_last = multiply(0, 1, 1)
         difference = multiply(1, 1, 1, also=(0,))
+        w1_last = multiply(0, 1, 1)
 
         round_weights(
             2,
@@ -173,8 +173,8 @@ def tile_picked_maxout_max_lo_kernel(tc, xT, w1, w2, w3, offs, out_0, out_1, out
 
         terms = keep.tile([P, 2, 2, HALF], F32, name="terms", tag=f"w_raw2_{W3_CUTS[2]}", align_bytes=64)
         held, excess = terms[:, 0], terms[:, 1]
-        nc.scalar.copy(out=held, in_=w1_last[:])
         nc.scalar.activation(excess, difference[:], mybir.ActivationFunctionType.Relu, scale=-1.0)
+        nc.scalar.copy(out=held, in_=w1_last[:])
         quantise_weights(2, ((0, 2), (2, 4)))
         last_max = keep.tile([P, 2, HALF], F32, name="last_max", tag="w_bf1", align_bytes=64)
         nc.gpsimd.tensor_tensor(last_max[:], held, excess, mybir.AluOpType.add)

@@ -26,7 +26,7 @@ LOADS = (((0, P),), tuple(zip(W2_CUTS, W2_CUTS[1:])), tuple(zip(W3_CUTS, W3_CUTS
 
 W1_SCALAR = 48
 
-BANKS = ((0, 1, 2, 0), (0, 1, 2, 4), (5, 6, 7, 1))
+BANKS = ((0, 1, 2, 0), (0, 1, 2, 4), (5, 6, 7, 3))
 
 
 def copy_on(nc, engine, out, in_, negate=False):
@@ -175,7 +175,7 @@ def tile_picked_maxout_max_lo_kernel(tc, xT, w1, w2, w3, offs, out_0, out_1, out
         held, excess = terms[:, 0], terms[:, 1]
         nc.scalar.activation(excess, difference[:], mybir.ActivationFunctionType.Relu, scale=-1.0)
         nc.scalar.copy(out=held, in_=w1_last[:])
-        quantise_weights(2, ((0, 2), (2, 4)))
+        quantise_weights(2, ((2, 4), (0, 2)))
         last_max = keep.tile([P, 2, HALF], F32, name="last_max", tag="w_bf1", align_bytes=64)
         nc.gpsimd.tensor_tensor(last_max[:], held, excess, mybir.AluOpType.add)
 
@@ -195,13 +195,12 @@ def tile_picked_maxout_max_lo_kernel(tc, xT, w1, w2, w3, offs, out_0, out_1, out
                 in_=y_bf[g][:].rearrange("p c r -> p (c r)"),
             )
 
-        w3_banks = {part: multiply(2, *part) for part in leading + ((1, 1),)}
-        for part in leading:
+        w3_banks = {part: multiply(2, *part) for part in ((0, 1), (1, 1), (0, 0), (1, 0))}
+        for part in ((0, 1), (0, 0), (1, 0)):
             nc.vector.tensor_tensor(pair(*part), w3_banks[part][:], pair(*part), MAX)
             store_rows(*part)
         interleave(nc, "scalar", y_bf[0][:], y[0])
-        for tokens in quarters[:2]:
-            nc.vector.tensor_tensor(pair(1, 1)[:, :, tokens], w3_banks[1, 1][:, :, tokens], last_max[:, :, tokens], MAX)
+        nc.vector.tensor_tensor(pair(1, 1), w3_banks[1, 1][:], last_max[:], MAX)
         store_rows(1, 1)
         interleave(nc, "scalar", y_bf[1][:], y[1][:, :, quarters[0]])
         quantise_result(0)

from contextlib import ExitStack

import concourse.mybir as mybir

K, T, S, N = 512, 1024, 512, 512
FLOPS = 3 * 2 * K * N * S

F32 = mybir.dt.float32
BF16 = mybir.dt.bfloat16
I32 = mybir.dt.int32
U32 = mybir.dt.uint32
U16 = mybir.dt.uint16
U8 = mybir.dt.uint8
FP8X4 = mybir.dt.float8_e4m3fn_x4
MAX = mybir.AluOpType.max

P = 128
PACK = 4
HALF = S // 2
QUARTER = S // 4
LIST_ROWS = 16

W2_CUTS = (0, 64, 96, P)
W3_CUTS = (0, 64, 96, P)
LOADS = (((0, P),), tuple(zip(W2_CUTS, W2_CUTS[1:])), tuple(zip(W3_CUTS, W3_CUTS[1:])))

W1_SCALAR = 48

BANKS = ((0, 1, 2, 0), (0, 1, 2, 4), (5, 6, 7, 3))


def copy_on(nc, engine, out, in_, negate=False):
    if negate and engine == "scalar":
        nc.scalar.mul(out, in_, -1.0)
    elif negate:
        nc.vector.tensor_scalar_mul(out, in_, -1.0)
    elif engine == "scalar":
        nc.scalar.copy(out=out, in_=in_)
    elif engine == "vector":
        nc.vector.tensor_copy(out=out, in_=in_)
    else:
        nc.gpsimd.tensor_scalar(out, in_, 1.0, 0.0, mybir.AluOpType.mult, mybir.AluOpType.add)


def interleave(nc, engine, grouped, planes):
    if engine == "gpsimd":
        copy_on(nc, engine, grouped, planes.rearrange("p r c -> p c r"))
    else:
        copy_on(
            nc, engine,
            grouped.rearrange("p (c i) r -> p c r i", i=4),
            planes.rearrange("p r (c i) -> p c r i", i=4),
        )


def tile_picked_maxout_max_lo_kernel(tc, xT, w1, w2, w3, offs, out_0, out_1, out_2):
    nc = tc.nc
    with ExitStack() as ctx:
        keep = ctx.enter_context(tc.tile_pool(name="keep", bufs=1))
        psum = ctx.enter_context(tc.psum_pool(name="psum", bufs=1))

        x_rows = xT.rearrange("(p r) t -> p r t", r=PACK)
        offsets = keep.tile([P, S // LIST_ROWS], U16, name="offsets")
        x_raw = [keep.tile([P, T], F32, name=f"x_raw{r}") for r in range(PACK)]
        w_raw = {}

        def load_weights(i, part):
            m0, m1 = LOADS[i][part]
            w_raw[i, m0] = keep.tile([P, PACK, PACK * (m1 - m0)], F32, name=f"w_raw{i}_{m0}", tag=f"w_raw{i}_{m0}", align_bytes=64)
            nc.sync.dma_start(w_raw[i, m0][:], (w1, w2, w3)[i].rearrange("(p r) n -> p r n", r=PACK)[:, :, PACK * m0 : PACK * m1])

        nc.sync.dma_start(x_raw[0][:], x_rows[:, 0, :])
        nc.sync.dma_start(offsets[:], offs)
        for r in range(1, PACK):
            nc.sync.dma_start(x_raw[r][:], x_rows[:, r, :])
        for i in range(3):
            for part in range(len(LOADS[i])):
                load_weights(i, part)

        picked = keep.tile([P, PACK, S], F32, name="picked")
        for r in range(PACK - 1):
            nc.vector.tensor_copy(picked[:, r, :], x_raw[r][:].indirect(offsets[:]))
        quarters = [slice(g * QUARTER, (g + 1) * QUARTER) for g in range(4)]
        for tokens in quarters:
            entries = offsets[:, tokens.start // LIST_ROWS : tokens.stop // LIST_ROWS]
            nc.vector.tensor_copy(picked[:, PACK - 1, tokens], x_raw[PACK - 1][:].indirect(entries))

        x_codes = {}
        x_scales = keep.tile([P, S], U8, name="x_scales", align_bytes=64)
        x_bf = keep.tile([P, S, PACK], BF16, name="x_bf", align_bytes=64)
        for tokens, engine in zip(quarters, ("scalar", "scalar", "vector", "vector")):
            interleave(nc, engine, x_bf[:, tokens, :], picked[:, :, tokens])

        def quantise_tokens(c, tag):
            tokens = slice(c * HALF, (c + 1) * HALF)
            x_codes[c] = keep.tile([P, HALF], U32, name=f"x_codes{c}", tag=tag, align_bytes=64)
            nc.vector.quantize_mx(
                out=x_codes[c][:].bitcast(FP8X4), scales=x_scales[:, tokens],
                in_=x_bf[:, tokens, :].rearrange("p c r -> p (c r)"),
            )

        quantise_tokens(0, "x_codes0")

        w_codes = [keep.tile([P, N], U32, name=f"w_codes{i}", align_bytes=64) for i in range(3)]
        w_scales = [keep.tile([P, N], U8, name=f"w_scales{i}", align_bytes=64) for i in range(3)]
        w_bf = {}

        def round_weights(i, shares, tag):
            w_bf[i] = keep.tile([P, PACK, P, PACK], BF16, name=f"w_bf{i}", tag=tag, align_bytes=64)
            for engine, m0, m1 in shares:
                first = max(start for start, stop in LOADS[i] if start <= m0)
                walk = "p m t r" if engine == "gpsimd" else "p m r t"
                copy_on(
                    nc, engine,
                    w_bf[i][:, :, m0:m1, :].rearrange(f"p t m r -> {walk}"),
                    w_raw[i, first][:, :, PACK * (m0 - first) : PACK * (m1 - first)].rearrange(f"p r (m t) -> {walk}", t=PACK),
                    negate=(i == 1),
                )

        def quantise_weights(i, calls):
            for t0, t1 in calls:
                cols = slice(t0 * P, t1 * P)
                nc.vector.quantize_mx(
                    out=w_codes[i][:, cols].bitcast(FP8X4), scales=w_scales[i][:, cols],
                    in_=w_bf[i][:, t0:t1].rearrange("p t m r -> p (t m r)"),
                )

        def multiply(i, c, u, also=()):
            bank = psum.tile([P, 2, HALF], F32, name=f"bank{i}{c}{u}", tag=f"bank{BANKS[i][2 * c + u]}")
            for e in range(2):
                cols = slice((2 * u + e) * P, (2 * u + e + 1) * P)
                terms = (i,) + also
                for j in terms:
                    nc.tensor.matmul_mx(
                        out=bank[:, e, :],
                        lhsT=w_codes[j][:, cols].bitcast(FP8X4),
                        lhsT_scale=w_scales[j][:, cols],
                        rhs=x_codes[c][:].bitcast(FP8X4),
                        rhs_scale=x_scales[:, c * HALF : (c + 1) * HALF],
                        start=(j == terms[0]), stop=(j == terms[-1]),
                    )
            return bank

        first_tiles_singly = ((0, 1), (1, 2), (2, 4))
        leading = ((0, 0), (0, 1), (1, 0))

        round_weights(0, [("scalar", 0, W1_SCALAR), ("vector", W1_SCALAR, P)], "w_bf0")
        quantise_weights(0, first_tiles_singly)
        quantise_tokens(1, "w_raw0_0")
        w1_banks = {part: multiply(0, *part) for part in leading}

        round_weights(1, [("scalar", 0, W2_CUTS[1]), ("vector", W2_CUTS[1], W2_CUTS[2]), ("vector", W2_CUTS[2], P)], "w_bf1")
        y_all = keep.tile([P, 2, PACK, HALF], F32, name="y_all", tag="w_raw1_0", align_bytes=64)
        y = [y_all[:, c] for c in range(2)]

        def pair(c, u):
            return y[c][:, 2 * u : 2 * u + 2, :]

        for part in leading:
            nc.scalar.copy(out=pair(*part), in_=w1_banks[part][:])
        quantise_weights(1, first_tiles_singly)
        w2_banks = {part: multiply(1, *part) for part in leading}
        difference = multiply(1, 1, 1, also=(0,))
        w1_last = multiply(0, 1, 1)

        round_weights(
            2,
            [("gpsimd", 0, W3_CUTS[1]), ("scalar", W3_CUTS[1], W3_CUTS[2]), ("scalar", W3_CUTS[2], P)],
            "w_bf1",
        )
        for part in leading:
            nc.vector.scalar_tensor_tensor(pair(*part), w2_banks[part][:], -1.0, pair(*part), mybir.AluOpType.mult, MAX)

        terms = keep.tile([P, 2, 2, HALF], F32, name="terms", tag=f"w_raw2_{W3_CUTS[2]}", align_bytes=64)
        held, excess = terms[:, 0], terms[:, 1]
        nc.scalar.activation(excess, difference[:], mybir.ActivationFunctionType.Relu, scale=-1.0)
        nc.scalar.copy(out=held, in_=w1_last[:])
        quantise_weights(2, ((2, 4), (0, 2)))
        last_max = keep.tile([P, 2, HALF], F32, name="last_max", tag="w_bf1", align_bytes=64)
        nc.gpsimd.tensor_tensor(last_max[:], held, excess, mybir.AluOpType.add)

        y_rows = out_0.rearrange("(p t) s -> p t s", t=PACK)
        y_codes = keep.tile([P, S], U32, name="y_codes", align_bytes=64)
        y_scales = keep.tile([P, S], U8, name="y_scales", align_bytes=64)
        pieces = (slice(0, HALF), quarters[2], quarters[3])
        y_bf = [keep.tile([P, tokens.stop - tokens.start, PACK], BF16, name=f"y_bf{g}", align_bytes=64) for g, tokens in enumerate(pieces)]
        words = out_1[0].rearrange("p s r -> p (s r)").bitcast(I32)

        def store_rows(c, u):
            nc.sync.dma_start(y_rows[:, 2 * u : 2 * u + 2, c * HALF : (c + 1) * HALF], pair(c, u))

        def quantise_result(g):
            nc.vector.quantize_mx(
                out=y_codes[:, pieces[g]].bitcast(FP8X4), scales=y_scales[:, pieces[g]],
                in_=y_bf[g][:].rearrange("p c r -> p (c r)"),
            )

        w3_banks = {part: multiply(2, *part) for part in ((0, 1), (1, 1), (0, 0), (1, 0))}
        for part in ((0, 1), (0, 0), (1, 0)):
            nc.vector.tensor_tensor(pair(*part), w3_banks[part][:], pair(*part), MAX)
            store_rows(*part)
        interleave(nc, "scalar", y_bf[0][:], y[0])
        nc.vector.tensor_tensor(pair(1, 1), w3_banks[1, 1][:], last_max[:], MAX)
        store_rows(1, 1)
        interleave(nc, "scalar", y_bf[1][:], y[1][:, :, quarters[0]])
        quantise_result(0)
        nc.sync.dma_start(words[:, 0:HALF], y_codes[:, 0:HALF].bitcast(I32))
        interleave(nc, "vector", y_bf[2][:], y[1][:, :, quarters[1]])
        quantise_result(1)
        quantise_result(2)
        nc.sync.dma_start(words[:, HALF:S], y_codes[:, HALF:S].bitcast(I32))

        for Q in range(4):
            queue = nc.scalar if Q % 2 == 0 else nc.sync
            queue.dma_start(out_2[0, 4 * Q : 4 * Q + 4, :].bitcast(I32), y_scales[32 * Q : 32 * Q + 4, :].bitcast(I32))
